import numpy as np
import ml_dtypes


def mxq(x, axis, fmt="e4m3"):
    dtype, down = {"e4m3": (ml_dtypes.float8_e4m3fn, 7), "e5m2": (ml_dtypes.float8_e5m2, 14)}[fmt]
    v = np.moveaxis(np.asarray(x, np.float32).astype(ml_dtypes.bfloat16).astype(np.float64), axis, -1)
    blocks = v.reshape(v.shape[:-1] + (-1, 32))
    amax = np.abs(blocks).max(-1, keepdims=True)
    byte = np.maximum(np.where(amax > 0, np.frexp(amax)[1] - 1 + 127, 0) - down, 1)
    scale = np.exp2(byte - 127.0)
    codes = (blocks / scale).astype(np.float32).astype(dtype).astype(np.float64)
    return np.moveaxis((codes * scale).reshape(v.shape), -1, axis)


WIDE = False


def mx_kscale(k):
    if not WIDE:
        return np.ones(k)
    levels = np.array([10, -10, 5, -5, 0])
    if k % 512:
        return np.exp2(np.random.permutation(np.resize(levels, k // 32))).repeat(32)
    a = np.empty((k // 512, 16))
    for p in range(k // 512):
        a[p, :8] = np.random.permutation(np.resize(levels, 8))
        for g in range(8):
            far = levels[np.abs(levels - a[p, g]) >= 10]
            a[p, g + 8] = far[np.random.randint(len(far))]
    return np.exp2(a.ravel()).repeat(32)


def f64(x):
    return np.asarray(x).astype(np.float64)


def striped(idx):
    return np.tile(idx.reshape(-1, 16).T, (8, 1)).astype(np.uint16)


def unstriped(offs):
    return offs[:16].T.reshape(-1).astype(np.int64)


E2M1 = np.array([0.0, 0.5, 1.0, 1.5, 2.0, 3.0, 4.0, 6.0, -0.0, -0.5, -1.0, -1.5, -2.0, -3.0, -4.0, -6.0])


def pack_fp4(w):
    k, n = w.shape
    w = f64(np.asarray(w, np.float32).astype(ml_dtypes.bfloat16)).reshape(k // 32, 32, n)
    amax = np.abs(w).max(1)
    mant, ex = np.frexp(amax / 6.0)
    byte = np.clip(np.where(amax > 0, np.where(mant > 0.5, ex, ex - 1) + 127, 1), 1, 254)
    scaled = (w * np.exp2(127.0 - byte)[:, None, :]).reshape(k, n).astype(np.float32)
    c = np.ascontiguousarray(scaled.reshape(k // 512, 128, 4, n).transpose(0, 1, 3, 2)).astype(ml_dtypes.float4_e2m1fn).view(np.uint8) & 0xF
    words = (c[..., 0::2] | (c[..., 1::2] << 4)).reshape(k // 512, 128, 2 * n)
    return np.ascontiguousarray(words), np.ascontiguousarray(byte.astype(np.uint8).reshape(k // 512, 16, n))


def unpack_fp4(words, scales):
    g, _, n = scales.shape
    words = np.ascontiguousarray(words).reshape(g, 128, n, 2)
    nib = np.empty((g, 128, n, 4), np.uint8)
    nib[..., 0::2] = words & 0xF
    nib[..., 1::2] = words >> 4
    vals = E2M1[nib] * np.repeat(np.exp2(scales.astype(np.float64) - 127.0), 8, axis=1)[..., None]
    return vals.transpose(0, 1, 3, 2).reshape(g * 512, n)


def sigmoid(v):
    return 1.0 / (1.0 + np.exp(-np.maximum(v, -700.0)))


K, T, S, V, N = 1024, 2048, 512, 256, 128


def setup_inputs():
    n = np.random.standard_normal
    s = mx_kscale(K)[:, None]
    packed_w1 = pack_fp4(n((K, N)) / np.sqrt(K) / s)
    return {
        "xT": (n((K, T)) * s).astype(np.float32),
        "w1_words": packed_w1[0],
        "w1_scales": packed_w1[1],
        "offs": striped(np.random.permutation(T)[:S]),
    }


def reference(xT, w1_words, w1_scales, offs):
    xq = mxq(f64(xT)[:, unstriped(offs)], 0, "e4m3")
    y = sigmoid(unpack_fp4(w1_words, w1_scales).T @ xq)
    return y[:, :V] * y[:, V:2 * V]

@@ -1,0 +1,86 @@
+from contextlib import ExitStack
+
+import concourse.mybir as mybir
+
+K, T, S, V, N = 1024, 2048, 512, 256, 128
+FLOPS = 2 * K * S * N
+
+F32 = mybir.dt.float32
+BF16 = mybir.dt.bfloat16
+I32 = mybir.dt.int32
+U32 = mybir.dt.uint32
+U16 = mybir.dt.uint16
+U8 = mybir.dt.uint8
+FP8X4 = mybir.dt.float8_e4m3fn_x4
+FP4X4 = mybir.dt.float4_e2m1fn_x4
+SIGMOID = mybir.ActivationFunctionType.Sigmoid
+
+P = 128
+PACK = 4
+PASSES = K // (P * PACK)
+PIECES = S // V
+HALF = 128
+HALVES = V // HALF
+
+
+def tile_picked_andpool_none_e_kernel(tc, xT, w1_words, w1_scales, offs, out):
+    nc = tc.nc
+    with ExitStack() as ctx:
+        keep = ctx.enter_context(tc.tile_pool(name="keep", bufs=1))
+        psum = ctx.enter_context(tc.psum_pool(name="psum", bufs=1))
+
+        offsets = keep.tile([P, S // 16], U16, name="offsets")
+        w_codes = keep.tile([P, PASSES, 2 * N], U8, name="w_codes", align_bytes=64)
+        w_scales = keep.tile([P, PASSES, N], U8, name="w_scales", align_bytes=64)
+        x_rows = xT.rearrange("(g p t) c -> g t p c", g=PASSES, t=PACK)
+        rows = [[keep.tile([P, T], F32, name="rows%d_%d" % (g, t)) for t in range(PACK)] for g in range(PASSES)]
+
+        nc.sync.dma_start(out=rows[0][0][:], in_=x_rows[0, 0])
+        nc.sync.dma_start(offsets[:], offs)
+        nc.vector.memset(w_scales[:].rearrange("p g n -> p (g n)").bitcast(I32), 0)
+        nc.scalar.dma_start(out=w_codes[:].bitcast(I32), in_=w1_words.rearrange("g p c -> p g c").bitcast(I32))
+        for q in range(4):
+            nc.scalar.dma_start(
+                out=w_scales[32 * q : 32 * q + 4].bitcast(I32),
+                in_=w1_scales[:, 4 * q : 4 * q + 4, :].rearrange("g r n -> r g n").bitcast(I32),
+            )
+        for g in range(PASSES):
+            for t in range(PACK):
+                if (g, t) != (0, 0):
+                    nc.sync.dma_start(out=rows[g][t][:], in_=x_rows[g, t])
+
+        acc = [[psum.tile([N, HALF], F32, name="acc%d_%d" % (d, h)) for h in range(HALVES)] for d in range(PIECES)]
+        for g in range(PASSES):
+            picked = [keep.tile([P, V, PACK], BF16, name="picked%d_%d" % (g, d), align_bytes=64) for d in range(PIECES)]
+            for t in range(PACK):
+                for d in range(PIECES):
+                    piece = offsets[:, d * (V // 16) : (d + 1) * (V // 16)]
+                    nc.vector.tensor_copy(picked[d][:, :, t], rows[g][t][:].indirect(piece))
+            for d in range(PIECES):
+                for h in range(HALVES):
+                    codes = keep.tile([P, HALF], U32, name="codes%d_%d_%d" % (g, d, h), align_bytes=64)
+                    scales = keep.tile([P, HALF], U8, name="scales%d_%d_%d" % (g, d, h), align_bytes=64)
+                    nc.vector.quantize_mx(
+                        out=codes[:].bitcast(FP8X4),
+                        scales=scales[:],
+                        in_=picked[d][:, h * HALF : (h + 1) * HALF, :].rearrange("p c t -> p (c t)"),
+                    )
+                    nc.tensor.matmul_mx(
+                        out=acc[d][h][:],
+                        lhsT=w_codes[:, g, :].bitcast(FP4X4),
+                        lhsT_scale=w_scales[:, g, :],
+                        rhs=codes[:].bitcast(FP8X4),
+                        rhs_scale=scales[:],
+                        start=(g == 0),
+                        stop=(g == PASSES - 1),
+                    )
+
+        truth = [[keep.tile([N, HALF], F32, name="truth%d_%d" % (d, h)) for h in range(HALVES)] for d in range(PIECES)]
+        for d in range(PIECES):
+            for h in range(HALVES):
+                nc.scalar.activation(truth[d][h][:], acc[d][h][:], SIGMOID)
+        for h in range(HALVES):
+            joined = keep.tile([N, HALF], F32, name="joined%d" % h)
+            nc.vector.tensor_mul(joined[:], truth[0][h][:], truth[1][h][:])
+            queue = nc.sync if h == 0 else nc.scalar
+            queue.dma_start(out=out[:, h * HALF : (h + 1) * HALF], in_=joined[:])

@@ -33,9 +33,11 @@ def tile_picked_andpool_none_e_kernel(tc, xT, w1_words, w1_scales, offs, out):
         w_codes = keep.tile([P, PASSES, 2 * N], U8, name="w_codes", align_bytes=64)
         w_scales = keep.tile([P, PASSES, N], U8, name="w_scales", align_bytes=64)
         x_rows = xT.rearrange("(g p t) c -> g t p c", g=PASSES, t=PACK)
-        rows = [[keep.tile([P, T], F32, name="rows%d_%d" % (g, t)) for t in range(PACK)] for g in range(PASSES)]
+        x_pairs = xT.rearrange("(g p u e) c -> g u p e c", g=PASSES, u=2, e=2)
+        pairs = [keep.tile([P, 2, T], F32, name="pair%d" % u) for u in range(2)]
+        rows = [keep.tile([P, T], F32, name="rows%d" % t, tag="rows%d" % t, align_bytes=64) for t in range(PACK)]
 
-        nc.sync.dma_start(out=rows[0][0][:], in_=x_rows[0, 0])
+        nc.sync.dma_start(out=pairs[0][:], in_=x_pairs[0, 0])
         nc.sync.dma_start(offsets[:], offs)
         nc.vector.memset(w_scales[:].rearrange("p g n -> p (g n)").bitcast(I32), 0)
         nc.scalar.dma_start(out=w_codes[:].bitcast(I32), in_=w1_words.rearrange("g p c -> p g c").bitcast(I32))
@@ -44,36 +46,60 @@ def tile_picked_andpool_none_e_kernel(tc, xT, w1_words, w1_scales, offs, out):
                 out=w_scales[32 * q : 32 * q + 4].bitcast(I32),
                 in_=w1_scales[:, 4 * q : 4 * q + 4, :].rearrange("g r n -> r g n").bitcast(I32),
             )
-        for g in range(PASSES):
-            for t in range(PACK):
-                if (g, t) != (0, 0):
-                    nc.sync.dma_start(out=rows[g][t][:], in_=x_rows[g, t])
+        nc.sync.dma_start(out=pairs[1][:], in_=x_pairs[0, 1])
+        for t in range(PACK):
+            nc.sync.dma_start(out=rows[t][:], in_=x_rows[1, t])
 
         acc = [[psum.tile([N, HALF], F32, name="acc%d_%d" % (d, h)) for h in range(HALVES)] for d in range(PIECES)]
-        for g in range(PASSES):
-            picked = [keep.tile([P, V, PACK], BF16, name="picked%d_%d" % (g, d), align_bytes=64) for d in range(PIECES)]
-            for t in range(PACK):
-                for d in range(PIECES):
-                    piece = offsets[:, d * (V // 16) : (d + 1) * (V // 16)]
-                    nc.vector.tensor_copy(picked[d][:, :, t], rows[g][t][:].indirect(piece))
+
+        def multiply(g, d, h, codes, scales):
+            nc.tensor.matmul_mx(
+                out=acc[d][h][:],
+                lhsT=w_codes[:, g, :].bitcast(FP4X4),
+                lhsT_scale=w_scales[:, g, :],
+                rhs=codes.bitcast(FP8X4),
+                rhs_scale=scales,
+                start=(g == 0),
+                stop=(g == PASSES - 1),
+            )
+
+        dense = keep.tile([P, PACK, S], F32, name="dense")
+        for t in range(PACK):
+            nc.vector.tensor_copy(dense[:, t, :], pairs[t // 2][:, t % 2, :].indirect(offsets[:]))
+        woven = keep.tile([P, S, PACK], BF16, name="woven", align_bytes=64)
+        nc.scalar.copy(
+            woven[:].rearrange("p (c i) t -> p c t i", i=4),
+            dense[:].rearrange("p t (c i) -> p c t i", i=4),
+        )
+
+        picked = [keep.tile([P, V, PACK], BF16, name="picked%d" % d, align_bytes=64) for d in range(PIECES)]
+
+        def gather(t):
             for d in range(PIECES):
-                for h in range(HALVES):
-                    codes = keep.tile([P, HALF], U32, name="codes%d_%d_%d" % (g, d, h), align_bytes=64)
-                    scales = keep.tile([P, HALF], U8, name="scales%d_%d_%d" % (g, d, h), align_bytes=64)
-                    nc.vector.quantize_mx(
-                        out=codes[:].bitcast(FP8X4),
-                        scales=scales[:],
-                        in_=picked[d][:, h * HALF : (h + 1) * HALF, :].rearrange("p c t -> p (c t)"),
-                    )
-                    nc.tensor.matmul_mx(
-                        out=acc[d][h][:],
-                        lhsT=w_codes[:, g, :].bitcast(FP4X4),
-                        lhsT_scale=w_scales[:, g, :],
-                        rhs=codes[:].bitcast(FP8X4),
-                        rhs_scale=scales[:],
-                        start=(g == 0),
-                        stop=(g == PASSES - 1),
-                    )
+                piece = offsets[:, d * (V // 16) : (d + 1) * (V // 16)]
+                nc.vector.tensor_copy(picked[d][:, :, t], rows[t][:].indirect(piece))
+
+        gather(0)
+        gather(1)
+        codes0 = keep.tile([P, S], U32, name="codes0", tag="rows1", align_bytes=64)
+        scales0 = keep.tile([P, S], U8, name="scales0", align_bytes=64)
+        nc.vector.quantize_mx(out=codes0[:].bitcast(FP8X4), scales=scales0[:], in_=woven[:].rearrange("p c t -> p (c t)"))
+        for d in range(PIECES):
+            for h in range(HALVES):
+                cols = slice(d * V + h * HALF, d * V + (h + 1) * HALF)
+                multiply(0, d, h, codes0[:, cols], scales0[:, cols])
+        gather(2)
+        gather(3)
+        for d in range(PIECES):
+            for h in range(HALVES):
+                codes = keep.tile([P, HALF], U32, name="codes%d_%d" % (d, h), align_bytes=64)
+                scales = keep.tile([P, HALF], U8, name="scales%d_%d" % (d, h), align_bytes=64)
+                nc.vector.quantize_mx(
+                    out=codes[:].bitcast(FP8X4),
+                    scales=scales[:],
+                    in_=picked[d][:, h * HALF : (h + 1) * HALF, :].rearrange("p c t -> p (c t)"),
+                )
+                multiply(1, d, h, codes[:], scales[:])
 
         truth = [[keep.tile([N, HALF], F32, name="truth%d_%d" % (d, h)) for h in range(HALVES)] for d in range(PIECES)]
         for d in range(PIECES):
@@ -82,5 +108,5 @@ def tile_picked_andpool_none_e_kernel(tc, xT, w1_words, w1_scales, offs, out):
         for h in range(HALVES):
             joined = keep.tile([N, HALF], F32, name="joined%d" % h)
             nc.vector.tensor_mul(joined[:], truth[0][h][:], truth[1][h][:])
-            queue = nc.sync if h == 0 else nc.scalar
+            queue = nc.scalar if h == 0 else nc.sync
             queue.dma_start(out=out[:, h * HALF : (h + 1) * HALF], in_=joined[:])

@@ -27,6 +27,7 @@ def tile_picked_andpool_none_e_kernel(tc, xT, w1_words, w1_scales, offs, out):
     nc = tc.nc
     with ExitStack() as ctx:
         keep = ctx.enter_context(tc.tile_pool(name="keep", bufs=1))
+        tail = ctx.enter_context(tc.tile_pool(name="tail", bufs=1))
         psum = ctx.enter_context(tc.psum_pool(name="psum", bufs=1))
 
         offsets = keep.tile([P, S // 16], U16, name="offsets")
@@ -63,6 +64,11 @@ def tile_picked_andpool_none_e_kernel(tc, xT, w1_words, w1_scales, offs, out):
                 stop=(g == PASSES - 1),
             )
 
+        warm_in = keep.tile([P, 1], F32, name="warm_in")
+        warm_out = keep.tile([P, 1], F32, name="warm_out")
+        nc.vector.memset(warm_in[:], 0.0)
+        nc.scalar.activation(warm_out[:], warm_in[:], SIGMOID)
+
         dense = keep.tile([P, PACK, S], F32, name="dense")
         for t in range(PACK):
             nc.vector.tensor_copy(dense[:, t, :], pairs[t // 2][:, t % 2, :].indirect(offsets[:]))
@@ -88,11 +94,27 @@ def tile_picked_andpool_none_e_kernel(tc, xT, w1_words, w1_scales, offs, out):
             for h in range(HALVES):
                 cols = slice(d * V + h * HALF, d * V + (h + 1) * HALF)
                 multiply(0, d, h, codes0[:, cols], scales0[:, cols])
-        gather(2)
-        gather(3)
+        late = tail.tile([P, HALVES, 2, HALF], BF16, name="late", align_bytes=64, offset=0)
+
+        def gather_late(t):
+            for h in range(HALVES):
+                part = offsets[:, h * (HALF // 16) : (h + 1) * (HALF // 16)]
+                nc.vector.tensor_copy(late[:, h, t - 2, :], rows[t][:].indirect(part))
+                if t == PACK - 1:
+                    nc.scalar.copy(
+                        picked[0][:, h * HALF : (h + 1) * HALF, 2:4],
+                        late[:, h].rearrange("p t c -> p c t"),
+                    )
+            nc.vector.tensor_copy(picked[1][:, :, t], rows[t][:].indirect(offsets[:, V // 16 : 2 * (V // 16)]))
+
+        gather_late(2)
+        gather_late(3)
         for d in range(PIECES):
             for h in range(HALVES):
-                codes = keep.tile([P, HALF], U32, name="codes%d_%d" % (d, h), align_bytes=64)
+                if d == 0:
+                    codes = keep.tile([P, HALF], U32, name="codes%d_%d" % (d, h), align_bytes=64)
+                else:
+                    codes = tail.tile([P, HALF], U32, name="codes%d_%d" % (d, h), align_bytes=64, offset=4 * HALF * h)
                 scales = keep.tile([P, HALF], U8, name="scales%d_%d" % (d, h), align_bytes=64)
                 nc.vector.quantize_mx(
                     out=codes[:].bitcast(FP8X4),

@@ -31,7 +31,6 @@ def tile_picked_andpool_none_e_kernel(tc, xT, w1_words, w1_scales, offs, out):
         psum = ctx.enter_context(tc.psum_pool(name="psum", bufs=1))
 
         offsets = keep.tile([P, S // 16], U16, name="offsets")
-        w_codes = keep.tile([P, PASSES, 2 * N], U8, name="w_codes", align_bytes=64)
         w_scales = keep.tile([P, PASSES, N], U8, name="w_scales", align_bytes=64)
         x_rows = xT.rearrange("(g p t) c -> g t p c", g=PASSES, t=PACK)
         x_pairs = xT.rearrange("(g p u e) c -> g u p e c", g=PASSES, u=2, e=2)
@@ -41,7 +40,6 @@ def tile_picked_andpool_none_e_kernel(tc, xT, w1_words, w1_scales, offs, out):
         nc.sync.dma_start(out=pairs[0][:], in_=x_pairs[0, 0])
         nc.sync.dma_start(offsets[:], offs)
         nc.vector.memset(w_scales[:].rearrange("p g n -> p (g n)").bitcast(I32), 0)
-        nc.scalar.dma_start(out=w_codes[:].bitcast(I32), in_=w1_words.rearrange("g p c -> p g c").bitcast(I32))
         for q in range(4):
             nc.scalar.dma_start(
                 out=w_scales[32 * q : 32 * q + 4].bitcast(I32),
@@ -53,7 +51,7 @@ def tile_picked_andpool_none_e_kernel(tc, xT, w1_words, w1_scales, offs, out):
 
         acc = [[psum.tile([N, HALF], F32, name="acc%d_%d" % (d, h)) for h in range(HALVES)] for d in range(PIECES)]
 
-        def multiply(g, d, h, codes, scales):
+        def multiply(w_codes, g, d, h, codes, scales):
             nc.tensor.matmul_mx(
                 out=acc[d][h][:],
                 lhsT=w_codes[:, g, :].bitcast(FP4X4),
@@ -90,25 +88,25 @@ def tile_picked_andpool_none_e_kernel(tc, xT, w1_words, w1_scales, offs, out):
         codes0 = keep.tile([P, S], U32, name="codes0", tag="rows1", align_bytes=64)
         scales0 = keep.tile([P, S], U8, name="scales0", align_bytes=64)
         nc.vector.quantize_mx(out=codes0[:].bitcast(FP8X4), scales=scales0[:], in_=woven[:].rearrange("p c t -> p (c t)"))
+
+        def gather_late(t, staged):
+            for h in range(HALVES):
+                part = offsets[:, h * (HALF // 16) : (h + 1) * (HALF // 16)]
+                nc.vector.tensor_copy(staged[h], rows[t][:].indirect(part))
+                nc.scalar.copy(picked[0][:, h * HALF : (h + 1) * HALF, t], staged[h])
+            nc.vector.tensor_copy(picked[1][:, :, t], rows[t][:].indirect(offsets[:, V // 16 : 2 * (V // 16)]))
+
+        mid0 = tail.tile([P, HALF], BF16, name="mid0", align_bytes=64, offset=8 * HALF)
+        mid1 = keep.tile([P, HALF], BF16, name="mid1", align_bytes=64)
+        gather_late(2, [mid0[:], mid1[:]])
+        w_codes = tail.tile([P, PASSES, 2 * N], U8, name="w_codes", align_bytes=64, offset=8 * HALF)
+        nc.scalar.dma_start(out=w_codes[:].bitcast(I32), in_=w1_words.rearrange("g p c -> p g c").bitcast(I32))
         for d in range(PIECES):
             for h in range(HALVES):
                 cols = slice(d * V + h * HALF, d * V + (h + 1) * HALF)
-                multiply(0, d, h, codes0[:, cols], scales0[:, cols])
-        late = tail.tile([P, HALVES, 2, HALF], BF16, name="late", align_bytes=64, offset=0)
-
-        def gather_late(t):
-            for h in range(HALVES):
-                part = offsets[:, h * (HALF // 16) : (h + 1) * (HALF // 16)]
-                nc.vector.tensor_copy(late[:, h, t - 2, :], rows[t][:].indirect(part))
-                if t == PACK - 1:
-                    nc.scalar.copy(
-                        picked[0][:, h * HALF : (h + 1) * HALF, 2:4],
-                        late[:, h].rearrange("p t c -> p c t"),
-                    )
-            nc.vector.tensor_copy(picked[1][:, :, t], rows[t][:].indirect(offsets[:, V // 16 : 2 * (V // 16)]))
-
-        gather_late(2)
-        gather_late(3)
+                multiply(w_codes, 0, d, h, codes0[:, cols], scales0[:, cols])
+        late = tail.tile([P, HALVES, HALF], BF16, name="late", align_bytes=64, offset=2 * HALF)
+        gather_late(3, [late[:, 0, :], late[:, 1, :]])
         for d in range(PIECES):
             for h in range(HALVES):
                 if d == 0:
@@ -121,7 +119,7 @@ def tile_picked_andpool_none_e_kernel(tc, xT, w1_words, w1_scales, offs, out):
                     scales=scales[:],
                     in_=picked[d][:, h * HALF : (h + 1) * HALF, :].rearrange("p c t -> p (c t)"),
                 )
-                multiply(1, d, h, codes[:], scales[:])
+                multiply(w_codes, 1, d, h, codes[:], scales[:])
 
         truth = [[keep.tile([N, HALF], F32, name="truth%d_%d" % (d, h)) for h in range(HALVES)] for d in range(PIECES)]
         for d in range(PIECES):

@@ -14,6 +14,7 @@ U8 = mybir.dt.uint8
 FP8X4 = mybir.dt.float8_e4m3fn_x4
 FP4X4 = mybir.dt.float4_e2m1fn_x4
 SIGMOID = mybir.ActivationFunctionType.Sigmoid
+COPY = mybir.ActivationFunctionType.Copy
 
 P = 128
 PACK = 4
@@ -21,6 +22,7 @@ PASSES = K // (P * PACK)
 PIECES = S // V
 HALF = 128
 HALVES = V // HALF
+RELEASE = 64
 
 
 def tile_picked_andpool_none_e_kernel(tc, xT, w1_words, w1_scales, offs, out):
@@ -36,6 +38,9 @@ def tile_picked_andpool_none_e_kernel(tc, xT, w1_words, w1_scales, offs, out):
         x_pairs = xT.rearrange("(g p u e) c -> g u p e c", g=PASSES, u=2, e=2)
         pairs = [keep.tile([P, 2, T], F32, name="pair%d" % u) for u in range(2)]
         rows = [keep.tile([P, T], F32, name="rows%d" % t, tag="rows%d" % t, align_bytes=64) for t in range(PACK)]
+
+        def entries(first, count):
+            return offsets[:, first // 16 : (first + count) // 16]
 
         nc.sync.dma_start(out=pairs[0][:], in_=x_pairs[0, 0])
         nc.sync.dma_start(offsets[:], offs)
@@ -78,53 +83,47 @@ def tile_picked_andpool_none_e_kernel(tc, xT, w1_words, w1_scales, offs, out):
 
         picked = [keep.tile([P, V, PACK], BF16, name="picked%d" % d, align_bytes=64) for d in range(PIECES)]
 
-        def gather(t):
+        for t in range(2):
             for d in range(PIECES):
-                piece = offsets[:, d * (V // 16) : (d + 1) * (V // 16)]
-                nc.vector.tensor_copy(picked[d][:, :, t], rows[t][:].indirect(piece))
-
-        gather(0)
-        gather(1)
+                nc.vector.tensor_copy(picked[d][:, :, t], rows[t][:].indirect(entries(d * V, V)))
         codes0 = keep.tile([P, S], U32, name="codes0", tag="rows1", align_bytes=64)
         scales0 = keep.tile([P, S], U8, name="scales0", align_bytes=64)
         nc.vector.quantize_mx(out=codes0[:].bitcast(FP8X4), scales=scales0[:], in_=woven[:].rearrange("p c t -> p (c t)"))
 
-        def gather_late(t, staged):
-            for h in range(HALVES):
-                part = offsets[:, h * (HALF // 16) : (h + 1) * (HALF // 16)]
-                nc.vector.tensor_copy(staged[h], rows[t][:].indirect(part))
-                nc.scalar.copy(picked[0][:, h * HALF : (h + 1) * HALF, t], staged[h])
-            nc.vector.tensor_copy(picked[1][:, :, t], rows[t][:].indirect(offsets[:, V // 16 : 2 * (V // 16)]))
+        def gather_shared(t, staged):
+            nc.vector.tensor_copy(picked[1][:, :, t], rows[t][:].indirect(entries(V, V)))
+            first = 0
+            for part in staged:
+                nc.scalar.activation(part[:], rows[t][:].indirect(entries(first, part.shape[1])), COPY)
+                first = first + part.shape[1]
+            first = 0
+            for part in staged:
+                nc.scalar.copy(picked[0][:, first : first + part.shape[1], t], part[:])
+                first = first + part.shape[1]
 
-        mid0 = tail.tile([P, HALF], BF16, name="mid0", align_bytes=64, offset=8 * HALF)
-        mid1 = keep.tile([P, HALF], BF16, name="mid1", align_bytes=64)
-        gather_late(2, [mid0[:], mid1[:]])
-        w_codes = tail.tile([P, PASSES, 2 * N], U8, name="w_codes", align_bytes=64, offset=8 * HALF)
+        mid0 = tail.tile([P, RELEASE], BF16, name="mid0", align_bytes=64, offset=0)
+        mid1 = keep.tile([P, V - RELEASE], BF16, name="mid1", align_bytes=64)
+        gather_shared(2, [mid0, mid1])
+        w_codes = tail.tile([P, PASSES, 2 * N], U8, name="w_codes", align_bytes=64, offset=0)
         nc.scalar.dma_start(out=w_codes[:].bitcast(I32), in_=w1_words.rearrange("g p c -> p g c").bitcast(I32))
-        for d in range(PIECES):
-            for h in range(HALVES):
-                cols = slice(d * V + h * HALF, d * V + (h + 1) * HALF)
-                multiply(w_codes, 0, d, h, codes0[:, cols], scales0[:, cols])
-        late = tail.tile([P, HALVES, HALF], BF16, name="late", align_bytes=64, offset=2 * HALF)
-        gather_late(3, [late[:, 0, :], late[:, 1, :]])
-        for d in range(PIECES):
-            for h in range(HALVES):
-                if d == 0:
-                    codes = keep.tile([P, HALF], U32, name="codes%d_%d" % (d, h), align_bytes=64)
-                else:
-                    codes = tail.tile([P, HALF], U32, name="codes%d_%d" % (d, h), align_bytes=64, offset=4 * HALF * h)
-                scales = keep.tile([P, HALF], U8, name="scales%d_%d" % (d, h), align_bytes=64)
-                nc.vector.quantize_mx(
-                    out=codes[:].bitcast(FP8X4),
-                    scales=scales[:],
-                    in_=picked[d][:, h * HALF : (h + 1) * HALF, :].rearrange("p c t -> p (c t)"),
-                )
-                multiply(w_codes, 1, d, h, codes[:], scales[:])
+        order = [(d, h) for d in (1, 0) for h in range(HALVES)]
+        for d, h in order:
+            cols = slice(d * V + h * HALF, d * V + (h + 1) * HALF)
+            multiply(w_codes, 0, d, h, codes0[:, cols], scales0[:, cols])
+        gather_shared(3, [keep.tile([P, HALF], BF16, name="late%d" % h, align_bytes=64) for h in range(HALVES)])
+        for d, h in order:
+            codes = keep.tile([P, HALF], U32, name="codes%d_%d" % (d, h), align_bytes=64)
+            scales = keep.tile([P, HALF], U8, name="scales%d_%d" % (d, h), align_bytes=64)
+            nc.vector.quantize_mx(
+                out=codes[:].bitcast(FP8X4),
+                scales=scales[:],
+                in_=picked[d][:, h * HALF : (h + 1) * HALF, :].rearrange("p c t -> p (c t)"),
+            )
+            multiply(w_codes, 1, d, h, codes[:], scales[:])
 
         truth = [[keep.tile([N, HALF], F32, name="truth%d_%d" % (d, h)) for h in range(HALVES)] for d in range(PIECES)]
-        for d in range(PIECES):
-            for h in range(HALVES):
-                nc.scalar.activation(truth[d][h][:], acc[d][h][:], SIGMOID)
+        for d, h in order:
+            nc.scalar.activation(truth[d][h][:], acc[d][h][:], SIGMOID)
         for h in range(HALVES):
             joined = keep.tile([N, HALF], F32, name="joined%d" % h)
             nc.vector.tensor_mul(joined[:], truth[0][h][:], truth[1][h][:])

@@ -22,14 +22,12 @@ PASSES = K // (P * PACK)
 PIECES = S // V
 HALF = 128
 HALVES = V // HALF
-RELEASE = 64
 
 
 def tile_picked_andpool_none_e_kernel(tc, xT, w1_words, w1_scales, offs, out):
     nc = tc.nc
     with ExitStack() as ctx:
         keep = ctx.enter_context(tc.tile_pool(name="keep", bufs=1))
-        tail = ctx.enter_context(tc.tile_pool(name="tail", bufs=1))
         psum = ctx.enter_context(tc.psum_pool(name="psum", bufs=1))
 
         offsets = keep.tile([P, S // 16], U16, name="offsets")
@@ -72,54 +70,34 @@ def tile_picked_andpool_none_e_kernel(tc, xT, w1_words, w1_scales, offs, out):
         nc.vector.memset(warm_in[:], 0.0)
         nc.scalar.activation(warm_out[:], warm_in[:], SIGMOID)
 
-        dense = keep.tile([P, PACK, S], F32, name="dense")
-        for t in range(PACK):
-            nc.vector.tensor_copy(dense[:, t, :], pairs[t // 2][:, t % 2, :].indirect(offsets[:]))
         woven = keep.tile([P, S, PACK], BF16, name="woven", align_bytes=64)
-        nc.scalar.copy(
-            woven[:].rearrange("p (c i) t -> p c t i", i=4),
-            dense[:].rearrange("p t (c i) -> p c t i", i=4),
-        )
-
-        picked = [keep.tile([P, V, PACK], BF16, name="picked%d" % d, align_bytes=64) for d in range(PIECES)]
-
-        for t in range(2):
-            for d in range(PIECES):
-                nc.vector.tensor_copy(picked[d][:, :, t], rows[t][:].indirect(entries(d * V, V)))
-        codes0 = keep.tile([P, S], U32, name="codes0", tag="rows1", align_bytes=64)
+        for t in range(PACK):
+            nc.vector.tensor_copy(woven[:, :, t], pairs[t // 2][:, t % 2, :].indirect(offsets[:]))
+        codes0 = keep.tile([P, S], U32, name="codes0", align_bytes=64)
         scales0 = keep.tile([P, S], U8, name="scales0", align_bytes=64)
         nc.vector.quantize_mx(out=codes0[:].bitcast(FP8X4), scales=scales0[:], in_=woven[:].rearrange("p c t -> p (c t)"))
 
-        def gather_shared(t, staged):
-            nc.vector.tensor_copy(picked[1][:, :, t], rows[t][:].indirect(entries(V, V)))
-            first = 0
-            for part in staged:
-                nc.scalar.activation(part[:], rows[t][:].indirect(entries(first, part.shape[1])), COPY)
-                first = first + part.shape[1]
-            first = 0
-            for part in staged:
-                nc.scalar.copy(picked[0][:, first : first + part.shape[1], t], part[:])
-                first = first + part.shape[1]
+        by_scalar = [keep.tile([P, HALF, PACK], BF16, name="by_scalar%d" % h, align_bytes=64) for h in range(HALVES)]
+        by_vector = keep.tile([P, V, PACK], BF16, name="by_vector", align_bytes=64)
+        for t in range(PACK):
+            nc.vector.tensor_copy(by_vector[:, :, t], rows[t][:].indirect(entries(V, V)))
+            for h in range(HALVES):
+                nc.scalar.activation(by_scalar[h][:, :, t], rows[t][:].indirect(entries(h * HALF, HALF)), COPY)
 
-        mid0 = tail.tile([P, RELEASE], BF16, name="mid0", align_bytes=64, offset=0)
-        mid1 = keep.tile([P, V - RELEASE], BF16, name="mid1", align_bytes=64)
-        gather_shared(2, [mid0, mid1])
-        w_codes = tail.tile([P, PASSES, 2 * N], U8, name="w_codes", align_bytes=64, offset=0)
+        w_codes = keep.tile([P, PASSES, 2 * N], U8, name="w_codes", tag="rows2", align_bytes=64)
         nc.scalar.dma_start(out=w_codes[:].bitcast(I32), in_=w1_words.rearrange("g p c -> p g c").bitcast(I32))
-        order = [(d, h) for d in (1, 0) for h in range(HALVES)]
+        order = [(0, 0), (1, 1), (1, 0), (0, 1)]
         for d, h in order:
             cols = slice(d * V + h * HALF, d * V + (h + 1) * HALF)
             multiply(w_codes, 0, d, h, codes0[:, cols], scales0[:, cols])
-        gather_shared(3, [keep.tile([P, HALF], BF16, name="late%d" % h, align_bytes=64) for h in range(HALVES)])
+        vector_codes = keep.tile([P, HALVES, HALF], U32, name="vector_codes", tag="rows3", align_bytes=64)
+        scalar_codes = keep.tile([P, HALVES, HALF], U32, name="scalar_codes", align_bytes=64)
         for d, h in order:
-            codes = keep.tile([P, HALF], U32, name="codes%d_%d" % (d, h), align_bytes=64)
+            codes = (scalar_codes if d == 0 else vector_codes)[:, h, :]
             scales = keep.tile([P, HALF], U8, name="scales%d_%d" % (d, h), align_bytes=64)
-            nc.vector.quantize_mx(
-                out=codes[:].bitcast(FP8X4),
-                scales=scales[:],
-                in_=picked[d][:, h * HALF : (h + 1) * HALF, :].rearrange("p c t -> p (c t)"),
-            )
-            multiply(w_codes, 1, d, h, codes[:], scales[:])
+            picked = by_scalar[h][:] if d == 0 else by_vector[:, h * HALF : (h + 1) * HALF, :]
+            nc.vector.quantize_mx(out=codes.bitcast(FP8X4), scales=scales[:], in_=picked.rearrange("p c t -> p (c t)"))
+            multiply(w_codes, 1, d, h, codes, scales[:])
 
         truth = [[keep.tile([N, HALF], F32, name="truth%d_%d" % (d, h)) for h in range(HALVES)] for d in range(PIECES)]
         for d, h in order:

@@ -77,16 +77,21 @@ def tile_picked_andpool_none_e_kernel(tc, xT, w1_words, w1_scales, offs, out):
         scales0 = keep.tile([P, S], U8, name="scales0", align_bytes=64)
         nc.vector.quantize_mx(out=codes0[:].bitcast(FP8X4), scales=scales0[:], in_=woven[:].rearrange("p c t -> p (c t)"))
 
-        by_scalar = [keep.tile([P, HALF, PACK], BF16, name="by_scalar%d" % h, align_bytes=64) for h in range(HALVES)]
-        by_vector = keep.tile([P, V, PACK], BF16, name="by_vector", align_bytes=64)
-        for t in range(PACK):
-            nc.vector.tensor_copy(by_vector[:, :, t], rows[t][:].indirect(entries(V, V)))
-            for h in range(HALVES):
-                nc.scalar.activation(by_scalar[h][:, :, t], rows[t][:].indirect(entries(h * HALF, HALF)), COPY)
+        picked = keep.tile([P, S, PACK], BF16, name="picked", align_bytes=64)
+
+        def scalar_gather(t, first, count):
+            nc.scalar.activation(picked[:, first : first + count, t], rows[t][:].indirect(entries(first, count)), COPY)
+
+        for t in range(2):
+            scalar_gather(t, 0, S)
+        for t, width in ((2, V), (3, HALF)):
+            nc.vector.tensor_copy(picked[:, V:, t], rows[t][:].indirect(entries(V, V)))
+            for first in range(0, V, width):
+                scalar_gather(t, first, width)
 
         w_codes = keep.tile([P, PASSES, 2 * N], U8, name="w_codes", tag="rows2", align_bytes=64)
         nc.scalar.dma_start(out=w_codes[:].bitcast(I32), in_=w1_words.rearrange("g p c -> p g c").bitcast(I32))
-        order = [(0, 0), (1, 1), (1, 0), (0, 1)]
+        order = [(d, h) for d in range(PIECES) for h in range(HALVES)]
         for d, h in order:
             cols = slice(d * V + h * HALF, d * V + (h + 1) * HALF)
             multiply(w_codes, 0, d, h, codes0[:, cols], scales0[:, cols])
@@ -95,8 +100,8 @@ def tile_picked_andpool_none_e_kernel(tc, xT, w1_words, w1_scales, offs, out):
         for d, h in order:
             codes = (scalar_codes if d == 0 else vector_codes)[:, h, :]
             scales = keep.tile([P, HALF], U8, name="scales%d_%d" % (d, h), align_bytes=64)
-            picked = by_scalar[h][:] if d == 0 else by_vector[:, h * HALF : (h + 1) * HALF, :]
-            nc.vector.quantize_mx(out=codes.bitcast(FP8X4), scales=scales[:], in_=picked.rearrange("p c t -> p (c t)"))
+            group = picked[:, d * V + h * HALF : d * V + (h + 1) * HALF, :]
+            nc.vector.quantize_mx(out=codes.bitcast(FP8X4), scales=scales[:], in_=group.rearrange("p c t -> p (c t)"))
             multiply(w_codes, 1, d, h, codes, scales[:])
 
         truth = [[keep.tile([N, HALF], F32, name="truth%d_%d" % (d, h)) for h in range(HALVES)] for d in range(PIECES)]

@@ -22,6 +22,8 @@ PASSES = K // (P * PACK)
 PIECES = S // V
 HALF = 128
 HALVES = V // HALF
+PART = 64
+SCALAR_THIRD = 224
 
 
 def tile_picked_andpool_none_e_kernel(tc, xT, w1_words, w1_scales, offs, out):
@@ -84,10 +86,14 @@ def tile_picked_andpool_none_e_kernel(tc, xT, w1_words, w1_scales, offs, out):
 
         for t in range(2):
             scalar_gather(t, 0, S)
-        for t, width in ((2, V), (3, HALF)):
-            nc.vector.tensor_copy(picked[:, V:, t], rows[t][:].indirect(entries(V, V)))
-            for first in range(0, V, width):
-                scalar_gather(t, first, width)
+        scalar_gather(2, 0, SCALAR_THIRD)
+        staged = keep.tile([P, S - SCALAR_THIRD], BF16, name="staged", align_bytes=64)
+        nc.vector.tensor_copy(staged[:], rows[2][:].indirect(entries(SCALAR_THIRD, S - SCALAR_THIRD)))
+        nc.scalar.copy(picked[:, SCALAR_THIRD:V, 2], staged[:, : V - SCALAR_THIRD])
+        nc.vector.tensor_copy(picked[:, V:, 2], staged[:, V - SCALAR_THIRD :])
+        nc.vector.tensor_copy(picked[:, V:, 3], rows[3][:].indirect(entries(V, V)))
+        for first, count in ((0, HALF), (HALF, PART), (HALF + PART, PART)):
+            scalar_gather(3, first, count)
 
         w_codes = keep.tile([P, PASSES, 2 * N], U8, name="w_codes", tag="rows2", align_bytes=64)
         nc.scalar.dma_start(out=w_codes[:].bitcast(I32), in_=w1_words.rearrange("g p c -> p g c").bitcast(I32))
@@ -100,8 +106,14 @@ def tile_picked_andpool_none_e_kernel(tc, xT, w1_words, w1_scales, offs, out):
         for d, h in order:
             codes = (scalar_codes if d == 0 else vector_codes)[:, h, :]
             scales = keep.tile([P, HALF], U8, name="scales%d_%d" % (d, h), align_bytes=64)
-            group = picked[:, d * V + h * HALF : d * V + (h + 1) * HALF, :]
-            nc.vector.quantize_mx(out=codes.bitcast(FP8X4), scales=scales[:], in_=group.rearrange("p c t -> p (c t)"))
+            width = PART if (d, h) == (0, 1) else HALF
+            for first in range(0, HALF, width):
+                start = d * V + h * HALF + first
+                nc.vector.quantize_mx(
+                    out=codes[:, first : first + width].bitcast(FP8X4),
+                    scales=scales[:, first : first + width],
+                    in_=picked[:, start : start + width, :].rearrange("p c t -> p (c t)"),
+                )
             multiply(w_codes, 1, d, h, codes, scales[:])
 
         truth = [[keep.tile([N, HALF], F32, name="truth%d_%d" % (d, h)) for h in range(HALVES)] for d in range(PIECES)]

from contextlib import ExitStack

import concourse.mybir as mybir

K, T, S, V, N = 1024, 2048, 512, 256, 128
FLOPS = 2 * K * S * N

F32 = mybir.dt.float32
BF16 = mybir.dt.bfloat16
I32 = mybir.dt.int32
U32 = mybir.dt.uint32
U16 = mybir.dt.uint16
U8 = mybir.dt.uint8
FP8X4 = mybir.dt.float8_e4m3fn_x4
FP4X4 = mybir.dt.float4_e2m1fn_x4
SIGMOID = mybir.ActivationFunctionType.Sigmoid
COPY = mybir.ActivationFunctionType.Copy

P = 128
PACK = 4
PASSES = K // (P * PACK)
PIECES = S // V
HALF = 128
HALVES = V // HALF
PART = 64
SCALAR_THIRD = 224


def tile_picked_andpool_none_e_kernel(tc, xT, w1_words, w1_scales, offs, out):
    nc = tc.nc
    with ExitStack() as ctx:
        keep = ctx.enter_context(tc.tile_pool(name="keep", bufs=1))
        psum = ctx.enter_context(tc.psum_pool(name="psum", bufs=1))

        offsets = keep.tile([P, S // 16], U16, name="offsets")
        w_scales = keep.tile([P, PASSES, N], U8, name="w_scales", align_bytes=64)
        x_rows = xT.rearrange("(g p t) c -> g t p c", g=PASSES, t=PACK)
        x_pairs = xT.rearrange("(g p u e) c -> g u p e c", g=PASSES, u=2, e=2)
        pairs = [keep.tile([P, 2, T], F32, name="pair%d" % u) for u in range(2)]
        rows = [keep.tile([P, T], F32, name="rows%d" % t, tag="rows%d" % t, align_bytes=64) for t in range(PACK)]

        def entries(first, count):
            return offsets[:, first // 16 : (first + count) // 16]

        nc.sync.dma_start(out=pairs[0][:], in_=x_pairs[0, 0])
        nc.sync.dma_start(offsets[:], offs)
        nc.vector.memset(w_scales[:].rearrange("p g n -> p (g n)").bitcast(I32), 0)
        for q in range(4):
            nc.scalar.dma_start(
                out=w_scales[32 * q : 32 * q + 4].bitcast(I32),
                in_=w1_scales[:, 4 * q : 4 * q + 4, :].rearrange("g r n -> r g n").bitcast(I32),
            )
        nc.sync.dma_start(out=pairs[1][:], in_=x_pairs[0, 1])
        for t in range(PACK):
            nc.sync.dma_start(out=rows[t][:], in_=x_rows[1, t])

        acc = [[psum.tile([N, HALF], F32, name="acc%d_%d" % (d, h)) for h in range(HALVES)] for d in range(PIECES)]

        def multiply(w_codes, g, d, h, codes, scales):
            nc.tensor.matmul_mx(
                out=acc[d][h][:],
                lhsT=w_codes[:, g, :].bitcast(FP4X4),
                lhsT_scale=w_scales[:, g, :],
                rhs=codes.bitcast(FP8X4),
                rhs_scale=scales,
                start=(g == 0),
                stop=(g == PASSES - 1),
            )

        warm_in = keep.tile([P, 1], F32, name="warm_in")
        warm_out = keep.tile([P, 1], F32, name="warm_out")
        nc.vector.memset(warm_in[:], 0.0)
        nc.scalar.activation(warm_out[:], warm_in[:], SIGMOID)

        woven = keep.tile([P, S, PACK], BF16, name="woven", align_bytes=64)
        for t in range(PACK):
            nc.vector.tensor_copy(woven[:, :, t], pairs[t // 2][:, t % 2, :].indirect(offsets[:]))
        codes0 = keep.tile([P, S], U32, name="codes0", align_bytes=64)
        scales0 = keep.tile([P, S], U8, name="scales0", align_bytes=64)
        nc.vector.quantize_mx(out=codes0[:].bitcast(FP8X4), scales=scales0[:], in_=woven[:].rearrange("p c t -> p (c t)"))

        picked = keep.tile([P, S, PACK], BF16, name="picked", align_bytes=64)

        def scalar_gather(t, first, count):
            nc.scalar.activation(picked[:, first : first + count, t], rows[t][:].indirect(entries(first, count)), COPY)

        for t in range(2):
            scalar_gather(t, 0, S)
        scalar_gather(2, 0, SCALAR_THIRD)
        staged = keep.tile([P, S - SCALAR_THIRD], BF16, name="staged", align_bytes=64)
        nc.vector.tensor_copy(staged[:], rows[2][:].indirect(entries(SCALAR_THIRD, S - SCALAR_THIRD)))
        nc.scalar.copy(picked[:, SCALAR_THIRD:V, 2], staged[:, : V - SCALAR_THIRD])
        nc.vector.tensor_copy(picked[:, V:, 2], staged[:, V - SCALAR_THIRD :])
        nc.vector.tensor_copy(picked[:, V:, 3], rows[3][:].indirect(entries(V, V)))
        for first, count in ((0, HALF), (HALF, PART), (HALF + PART, PART)):
            scalar_gather(3, first, count)

        w_codes = keep.tile([P, PASSES, 2 * N], U8, name="w_codes", tag="rows2", align_bytes=64)
        nc.scalar.dma_start(out=w_codes[:].bitcast(I32), in_=w1_words.rearrange("g p c -> p g c").bitcast(I32))
        order = [(d, h) for d in range(PIECES) for h in range(HALVES)]
        for d, h in order:
            cols = slice(d * V + h * HALF, d * V + (h + 1) * HALF)
            multiply(w_codes, 0, d, h, codes0[:, cols], scales0[:, cols])
        vector_codes = keep.tile([P, HALVES, HALF], U32, name="vector_codes", tag="rows3", align_bytes=64)
        scalar_codes = keep.tile([P, HALVES, HALF], U32, name="scalar_codes", align_bytes=64)
        for d, h in order:
            codes = (scalar_codes if d == 0 else vector_codes)[:, h, :]
            scales = keep.tile([P, HALF], U8, name="scales%d_%d" % (d, h), align_bytes=64)
            width = PART if (d, h) == (0, 1) else HALF
            for first in range(0, HALF, width):
                start = d * V + h * HALF + first
                nc.vector.quantize_mx(
                    out=codes[:, first : first + width].bitcast(FP8X4),
                    scales=scales[:, first : first + width],
                    in_=picked[:, start : start + width, :].rearrange("p c t -> p (c t)"),
                )
            multiply(w_codes, 1, d, h, codes, scales[:])

        truth = [[keep.tile([N, HALF], F32, name="truth%d_%d" % (d, h)) for h in range(HALVES)] for d in range(PIECES)]
        for d, h in order:
            nc.scalar.activation(truth[d][h][:], acc[d][h][:], SIGMOID)
        for h in range(HALVES):
            joined = keep.tile([N, HALF], F32, name="joined%d" % h)
            nc.vector.tensor_mul(joined[:], truth[0][h][:], truth[1][h][:])
            queue = nc.scalar if h == 0 else nc.sync
            queue.dma_start(out=out[:, h * HALF : (h + 1) * HALF], in_=joined[:])
